import numpy as np
import ml_dtypes


def mxq(x, axis, fmt="e4m3"):
    dtype, down = {"e4m3": (ml_dtypes.float8_e4m3fn, 7), "e5m2": (ml_dtypes.float8_e5m2, 14)}[fmt]
    v = np.moveaxis(np.asarray(x, np.float32).astype(ml_dtypes.bfloat16).astype(np.float64), axis, -1)
    blocks = v.reshape(v.shape[:-1] + (-1, 32))
    amax = np.abs(blocks).max(-1, keepdims=True)
    byte = np.maximum(np.where(amax > 0, np.frexp(amax)[1] - 1 + 127, 0) - down, 1)
    scale = np.exp2(byte - 127.0)
    codes = (blocks / scale).astype(np.float32).astype(dtype).astype(np.float64)
    return np.moveaxis((codes * scale).reshape(v.shape), -1, axis)


WIDE = False


def mx_kscale(k, group=512):
    if not WIDE:
        return np.ones(k)
    levels = np.array([18, -18])
    if group != 512:
        return np.exp2(np.random.permutation(np.resize(levels, k // group))).repeat(group)
    if k % 512:
        return np.exp2(np.random.permutation(np.resize(levels, k // 32))).repeat(32)
    a = np.empty((k // 512, 16))
    for p in range(k // 512):
        a[p, :8] = np.random.permutation(np.resize(levels, 8))
        for g in range(8):
            far = levels[np.abs(levels - a[p, g]) >= 10]
            a[p, g + 8] = far[np.random.randint(len(far))]
    return np.exp2(a.ravel()).repeat(32)


def f64(x):
    return np.asarray(x).astype(np.float64)


def sigmoid(v):
    return 1.0 / (1.0 + np.exp(-v))


def bf(x):
    return np.asarray(x, np.float32).astype(ml_dtypes.bfloat16)


def planes(Y):
    r, m = Y.shape
    b = f64(bf(Y)).reshape(r // 32, 32, m)
    amax = np.abs(b).max(1)
    byte = np.clip(np.where(amax > 0, np.frexp(amax)[1] - 1 + 127 - 7, 1), 1, 254)
    codes = (b * np.exp2(127.0 - byte)[:, None, :]).reshape(r, m).astype(np.float32).astype(ml_dtypes.float8_e4m3fn).view(np.uint8)
    words = codes.reshape(r // 512, 128, 4, m).transpose(0, 1, 3, 2)
    return np.ascontiguousarray(words), np.ascontiguousarray(byte.astype(np.uint8).reshape(r // 512, 16, m))


G, D, M, N = 4, 128, 128, 512


def setup_inputs():
    n = np.random.standard_normal
    s_d = mx_kscale(D, 0)
    return {
        "h": (n((G, D, N)) * s_d[:, None]).astype(np.float32),
        "wr": (n((G, D, M)) / np.sqrt(D) / s_d[:, None]).astype(np.float32),
        "wu": (n((G, D, M)) / np.sqrt(D) / s_d[:, None]).astype(np.float32),
        "wc": (n((G, D, M)) / np.sqrt(D) / s_d[:, None]).astype(np.float32),
        "xr": (n((G, M, N))).astype(np.float32),
        "xu": (n((G, M, N))).astype(np.float32),
        "xc": (n((G, M, N))).astype(np.float32),
        "hp": (n((G, M, N))).astype(np.float32),
        "bc": (0.5 * n((G, M, 1))).astype(np.float32),
    }


def reference(h, wr, wu, wc, xr, xu, xc, hp, bc):
    wrq = mxq(f64(wr), 1, "e4m3")
    hq = mxq(f64(h), 1, "e4m3")
    zr = wrq.transpose(0, 2, 1) @ hq
    wuq = mxq(f64(wu), 1, "e4m3")
    zu = wuq.transpose(0, 2, 1) @ hq
    wcq = mxq(f64(wc), 1, "e4m3")
    zc = wcq.transpose(0, 2, 1) @ hq
    u = sigmoid(zu + f64(xu))
    cd = np.tanh(f64(xc) + sigmoid(zr + f64(xr)) * (zc + f64(bc)))
    y = (1.0 - u) * cd + u * f64(hp)
    Y = y.reshape(G * M, N)
    words, scales = planes(Y)
    return Y, words, scales

@@ -1,0 +1,212 @@
+from contextlib import ExitStack
+
+import concourse.mybir as mybir
+
+G, D, M, N = 4, 128, 128, 512
+FLOPS = 3 * 2 * G * D * M * N
+
+F32 = mybir.dt.float32
+BF16 = mybir.dt.bfloat16
+I32 = mybir.dt.int32
+U32 = mybir.dt.uint32
+U8 = mybir.dt.uint8
+FP8X4 = mybir.dt.float8_e4m3fn_x4
+ALU = mybir.AluOpType
+ACT = mybir.ActivationFunctionType
+
+P = 128
+PACK = 4
+ROWS = D // PACK
+HALF = N // 2
+H_SPLIT = 352
+
+UNITS = [(0, 0, N), (1, 0, N), (2, 0, N), (3, 0, 256), (3, 256, 384), (3, 384, 512)]
+
+
+def interleave(copy, grouped, raw, c0, c1, at):
+    width = c1 - c0
+    dst = grouped[:, PACK * at : PACK * (at + width)].rearrange("p (c i j) -> p c j i", i=4, j=PACK)
+    src = raw[:, :, c0:c1].rearrange("p j (c i) -> p c j i", i=4)
+    copy(out=dst, in_=src)
+
+
+def tile_rows_pl_cell_gru_kernel(tc, h, wr, wu, wc, xr, xu, xc, hp, bc, out_0, out_1, out_2):
+    nc = tc.nc
+    with ExitStack() as ctx:
+        sb = ctx.enter_context(tc.tile_pool(name="sb", bufs=1))
+        ps = ctx.enter_context(tc.psum_pool(name="ps", bufs=1))
+        ctx.enter_context(tc.manual_schedule())
+
+        def tile(name, shape, dtype):
+            return sb.tile(shape, dtype, name=name, align_bytes=64)
+
+        def per_group(name):
+            return [tile("%s%d" % (name, g), [P, N], F32) for g in range(G)]
+
+        def quantize(codes, scales, grouped, c0, c1, at):
+            nc.vector.quantize_mx(
+                out=codes[:, c0:c1].bitcast(FP8X4),
+                scales=scales[:, c0:c1],
+                in_=grouped[:, PACK * at : PACK * (at + c1 - c0)],
+            )
+
+        h_raw = tile("h_raw", [P, PACK, N], F32)
+        w_raw = {name: tile(name + "_raw", [P, PACK, M], F32) for name in ("wr", "wc", "wu")}
+        w_src = {"wr": wr, "wc": wc, "wu": wu}
+        x_src = {"xr": xr, "xu": xu, "xc": xc, "hp": hp}
+        x_sb = {name: per_group(name) for name in x_src}
+
+        def load_w(name):
+            nc.sync.dma_start(out=w_raw[name][:], in_=w_src[name].rearrange("g (p j) m -> (g p) j m", j=PACK))
+
+        def load_x(name, g):
+            nc.sync.dma_start(out=x_sb[name][g][:], in_=x_src[name][g])
+
+        load_w("wr")
+        nc.sync.dma_start(out=h_raw[:], in_=h.rearrange("g (p j) n -> (g p) j n", j=PACK))
+        load_w("wc")
+        load_x("xr", 0)
+        load_w("wu")
+        load_x("xr", 1)
+        load_x("xu", 0)
+        for g in range(G):
+            load_x("xc", g)
+            if g + 2 < G:
+                load_x("xr", g + 2)
+            if g + 1 < G:
+                load_x("xu", g + 1)
+            load_x("hp", g)
+
+        bias_rows = tile("bias_rows", [P, P], F32)
+        bias_cols = tile("bias_cols", [P, P], F32)
+        nc.vector.memset(bias_rows[:], 0.0)
+        nc.scalar.dma_start(
+            out=bias_rows[0:P:32, :].rearrange("q (g i) -> q g i", g=G),
+            in_=bc.rearrange("g (q i) o -> q g (i o)", i=32),
+        )
+
+        warm_in = tile("warm_in", [P, 1], F32)
+        warm_out = tile("warm_out", [P, 1], F32)
+        nc.vector.memset(warm_in[:], 0.0)
+        nc.scalar.activation(out=warm_out[:], in_=warm_in[:], func=ACT.Sigmoid)
+
+        w_bf = {name: tile(name + "_bf", [P, PACK * M], BF16) for name in w_raw}
+        w_codes = {name: tile(name + "_codes", [P, M], U32) for name in w_raw}
+        w_scales = {name: tile(name + "_scales", [P, M], U8) for name in w_raw}
+        h_bf = [tile("h_bf%d" % i, [P, PACK * HALF], BF16) for i in range(2)]
+        h_codes = tile("h_codes", [P, N], U32)
+        h_scales = tile("h_scales", [P, N], U8)
+
+        def quantize_w(name):
+            quantize(w_codes[name], w_scales[name], w_bf[name], 0, M, 0)
+
+        interleave(nc.vector.tensor_copy, w_bf["wr"], w_raw["wr"], 0, M, 0)
+        quantize_w("wr")
+        interleave(nc.scalar.copy, h_bf[1], h_raw, H_SPLIT, N, H_SPLIT - HALF)
+        interleave(nc.vector.tensor_copy, h_bf[0], h_raw, 0, HALF, 0)
+        interleave(nc.vector.tensor_copy, h_bf[1], h_raw, HALF, H_SPLIT, 0)
+        quantize(h_codes, h_scales, h_bf[0], 0, HALF, 0)
+        quantize(h_codes, h_scales, h_bf[1], HALF, N, 0)
+        interleave(nc.scalar.copy, w_bf["wc"], w_raw["wc"], 0, M, 0)
+        interleave(nc.scalar.copy, w_bf["wu"], w_raw["wu"], 0, M, 0)
+
+        gate_bank = [ps.tile([P, N], F32, name="gate_bank%d" % g) for g in range(G)]
+        cand_bank = [ps.tile([P, N], F32, name="cand_bank%d" % g) for g in range(G)]
+
+        def product(bank, name, g):
+            rows = slice(ROWS * g, ROWS * (g + 1))
+            nc.tensor.matmul_mx(
+                out=bank[g][:],
+                lhsT=w_codes[name][rows, :].bitcast(FP8X4),
+                lhsT_scale=w_scales[name][rows, :],
+                rhs=h_codes[rows, :].bitcast(FP8X4),
+                rhs_scale=h_scales[rows, :],
+                start=True,
+                stop=True,
+            )
+
+        for g in range(G):
+            product(gate_bank, "wr", g)
+        nc.vector.transpose(out=bias_cols[:], in_=bias_rows[:])
+        quantize_w("wc")
+        for g in range(G):
+            product(cand_bank, "wc", g)
+
+        r_sum, r, u_sum, u = per_group("r_sum"), per_group("r"), per_group("u_sum"), per_group("u")
+        gated, c_sum, cand = per_group("gated"), per_group("c_sum"), per_group("cand")
+        kept, fresh, y = per_group("kept"), per_group("fresh"), per_group("y")
+        moved = [tile("moved%d" % i, [P, PACK, HALF], F32) for i in range(2)]
+
+        def reset_gate(g):
+            nc.vector.tensor_tensor(out=r_sum[g][:], in0=gate_bank[g][:], in1=x_sb["xr"][g][:], op=ALU.add)
+            nc.scalar.activation(out=r[g][:], in_=r_sum[g][:], func=ACT.Sigmoid)
+
+        def update_gate(g):
+            nc.vector.tensor_tensor(out=u_sum[g][:], in0=gate_bank[g][:], in1=x_sb["xu"][g][:], op=ALU.add)
+            nc.scalar.activation(out=u[g][:], in_=u_sum[g][:], func=ACT.Sigmoid)
+
+        def apply_reset(g, c0, c1):
+            nc.vector.scalar_tensor_tensor(
+                out=gated[g][:, c0:c1], in0=cand_bank[g][:, c0:c1], scalar=bias_cols[:, 32 * g : 32 * g + 1],
+                in1=r[g][:, c0:c1], op0=ALU.add, op1=ALU.mult,
+            )
+
+        def candidate(g, c0, c1):
+            nc.vector.tensor_tensor(out=c_sum[g][:, c0:c1], in0=gated[g][:, c0:c1], in1=x_sb["xc"][g][:, c0:c1], op=ALU.add)
+            nc.scalar.activation(out=cand[g][:, c0:c1], in_=c_sum[g][:, c0:c1], func=ACT.Tanh)
+
+        def mix_parts(g, c0, c1):
+            nc.vector.tensor_tensor(out=kept[g][:, c0:c1], in0=u[g][:, c0:c1], in1=x_sb["hp"][g][:, c0:c1], op=ALU.mult)
+            nc.vector.scalar_tensor_tensor(
+                out=fresh[g][:, c0:c1], in0=u[g][:, c0:c1], scalar=1.0, in1=cand[g][:, c0:c1],
+                op0=ALU.subtract, op1=ALU.mult,
+            )
+
+        def finish(g, c0, c1):
+            nc.vector.tensor_tensor(out=y[g][:, c0:c1], in0=kept[g][:, c0:c1], in1=fresh[g][:, c0:c1], op=ALU.subtract)
+            for i in range(2):
+                lo, hi = max(c0, HALF * i), min(c1, HALF * (i + 1))
+                if lo < hi:
+                    nc.sync.dma_start(
+                        out=moved[i][ROWS * g : ROWS * (g + 1), :, lo - HALF * i : hi - HALF * i], in_=y[g][:, lo:hi]
+                    )
+            nc.sync.dma_start(out=out_0[M * g : M * (g + 1), c0:c1], in_=y[g][:, c0:c1])
+
+        reset_gate(0)
+        quantize_w("wu")
+        product(gate_bank, "wu", 0)
+        reset_gate(1)
+        product(gate_bank, "wu", 1)
+        apply_reset(*UNITS[0])
+        update_gate(0)
+        for i, unit in enumerate(UNITS):
+            candidate(*unit)
+            if i > 0:
+                finish(*UNITS[i - 1])
+            if i + 2 < G:
+                reset_gate(i + 2)
+                product(gate_bank, "wu", i + 2)
+            if i + 1 < len(UNITS):
+                apply_reset(*UNITS[i + 1])
+            if i + 1 < G:
+                update_gate(i + 1)
+            mix_parts(*unit)
+        finish(*UNITS[-1])
+
+        y_bf = [tile("y_bf%d" % i, [P, PACK * HALF], BF16) for i in range(2)]
+        y_codes = tile("y_codes", [P, N], U32)
+        y_scales = tile("y_scales", [P, N], U8)
+        words = out_1.rearrange("s p n x -> (s p) (n x)").bitcast(I32)
+        scale_rows = out_2.rearrange("s f n -> (s f) n").bitcast(I32)
+
+        interleave(nc.vector.tensor_copy, y_bf[0], moved[0], 0, HALF, 0)
+        quantize(y_codes, y_scales, y_bf[0], 0, HALF, 0)
+        nc.sync.dma_start(out=words[:, 0:HALF], in_=y_codes[:, 0:HALF].bitcast(I32))
+        interleave(nc.vector.tensor_copy, y_bf[1], moved[1], 0, 128, 0)
+        interleave(nc.vector.tensor_copy, y_bf[1], moved[1], 128, HALF, 128)
+        quantize(y_codes, y_scales, y_bf[1], HALF, HALF + 128, 0)
+        quantize(y_codes, y_scales, y_bf[1], HALF + 128, N, 128)
+        nc.sync.dma_start(out=words[:, HALF:N], in_=y_codes[:, HALF:N].bitcast(I32))
+        for q in range(4):
+            queue = nc.scalar if q < 2 else nc.sync
+            queue.dma_start(out=scale_rows[4 * q : 4 * q + 4, :], in_=y_scales[32 * q : 32 * q + 4, :].bitcast(I32))

@@ -18,9 +18,7 @@ P = 128
 PACK = 4
 ROWS = D // PACK
 HALF = N // 2
-H_SPLIT = 352
-
-UNITS = [(0, 0, N), (1, 0, N), (2, 0, N), (3, 0, 256), (3, 256, 384), (3, 384, 512)]
+H_SPLIT = 416
 
 
 def interleave(copy, grouped, raw, c0, c1, at):
@@ -62,20 +60,22 @@ def tile_rows_pl_cell_gru_kernel(tc, h, wr, wu, wc, xr, xu, xc, hp, bc, out_0, o
         def load_x(name, g):
             nc.sync.dma_start(out=x_sb[name][g][:], in_=x_src[name][g])
 
-        load_w("wr")
         nc.sync.dma_start(out=h_raw[:], in_=h.rearrange("g (p j) n -> (g p) j n", j=PACK))
+        load_w("wr")
         load_w("wc")
         load_x("xr", 0)
-        load_w("wu")
         load_x("xr", 1)
-        load_x("xu", 0)
-        for g in range(G):
-            load_x("xc", g)
+        load_w("wu")
+        load_x("xc", 0)
+        for g in range(G - 1):
             if g + 2 < G:
                 load_x("xr", g + 2)
-            if g + 1 < G:
+            load_x("xu", g)
+            if g + 2 == G:
                 load_x("xu", g + 1)
+            load_x("xc", g + 1)
             load_x("hp", g)
+        load_x("hp", G - 1)
 
         bias_rows = tile("bias_rows", [P, P], F32)
         bias_cols = tile("bias_cols", [P, P], F32)
@@ -100,15 +100,16 @@ def tile_rows_pl_cell_gru_kernel(tc, h, wr, wu, wc, xr, xu, xc, hp, bc, out_0, o
         def quantize_w(name):
             quantize(w_codes[name], w_scales[name], w_bf[name], 0, M, 0)
 
-        interleave(nc.vector.tensor_copy, w_bf["wr"], w_raw["wr"], 0, M, 0)
-        quantize_w("wr")
+        nc.vector.transpose(out=bias_cols[:], in_=bias_rows[:])
         interleave(nc.scalar.copy, h_bf[1], h_raw, H_SPLIT, N, H_SPLIT - HALF)
+        interleave(nc.scalar.copy, w_bf["wr"], w_raw["wr"], 0, M, 0)
+        interleave(nc.scalar.copy, w_bf["wc"], w_raw["wc"], 0, M, 0)
+        interleave(nc.scalar.copy, w_bf["wu"], w_raw["wu"], 0, M, 0)
         interleave(nc.vector.tensor_copy, h_bf[0], h_raw, 0, HALF, 0)
         interleave(nc.vector.tensor_copy, h_bf[1], h_raw, HALF, H_SPLIT, 0)
         quantize(h_codes, h_scales, h_bf[0], 0, HALF, 0)
         quantize(h_codes, h_scales, h_bf[1], HALF, N, 0)
-        interleave(nc.scalar.copy, w_bf["wc"], w_raw["wc"], 0, M, 0)
-        interleave(nc.scalar.copy, w_bf["wu"], w_raw["wu"], 0, M, 0)
+        quantize_w("wr")
 
         gate_bank = [ps.tile([P, N], F32, name="gate_bank%d" % g) for g in range(G)]
         cand_bank = [ps.tile([P, N], F32, name="cand_bank%d" % g) for g in range(G)]
@@ -127,7 +128,6 @@ def tile_rows_pl_cell_gru_kernel(tc, h, wr, wu, wc, xr, xu, xc, hp, bc, out_0, o
 
         for g in range(G):
             product(gate_bank, "wr", g)
-        nc.vector.transpose(out=bias_cols[:], in_=bias_rows[:])
         quantize_w("wc")
         for g in range(G):
             product(cand_bank, "wc", g)
@@ -145,25 +145,29 @@ def tile_rows_pl_cell_gru_kernel(tc, h, wr, wu, wc, xr, xu, xc, hp, bc, out_0, o
             nc.vector.tensor_tensor(out=u_sum[g][:], in0=gate_bank[g][:], in1=x_sb["xu"][g][:], op=ALU.add)
             nc.scalar.activation(out=u[g][:], in_=u_sum[g][:], func=ACT.Sigmoid)
 
-        def apply_reset(g, c0, c1):
+        def apply_reset(g):
             nc.vector.scalar_tensor_tensor(
-                out=gated[g][:, c0:c1], in0=cand_bank[g][:, c0:c1], scalar=bias_cols[:, 32 * g : 32 * g + 1],
-                in1=r[g][:, c0:c1], op0=ALU.add, op1=ALU.mult,
+                out=gated[g][:], in0=cand_bank[g][:], scalar=bias_cols[:, 32 * g : 32 * g + 1],
+                in1=r[g][:], op0=ALU.add, op1=ALU.mult,
             )
 
-        def candidate(g, c0, c1):
-            nc.vector.tensor_tensor(out=c_sum[g][:, c0:c1], in0=gated[g][:, c0:c1], in1=x_sb["xc"][g][:, c0:c1], op=ALU.add)
-            nc.scalar.activation(out=cand[g][:, c0:c1], in_=c_sum[g][:, c0:c1], func=ACT.Tanh)
+        def candidate_sum(engine, g):
+            engine.tensor_tensor(out=c_sum[g][:], in0=gated[g][:], in1=x_sb["xc"][g][:], op=ALU.add)
 
-        def mix_parts(g, c0, c1):
-            nc.vector.tensor_tensor(out=kept[g][:, c0:c1], in0=u[g][:, c0:c1], in1=x_sb["hp"][g][:, c0:c1], op=ALU.mult)
+        def candidate(g):
+            nc.scalar.activation(out=cand[g][:], in_=c_sum[g][:], func=ACT.Tanh)
+
+        def kept_part(g):
+            nc.vector.tensor_tensor(out=kept[g][:], in0=u[g][:], in1=x_sb["hp"][g][:], op=ALU.mult)
+
+        def fresh_part(g, c0, c1):
             nc.vector.scalar_tensor_tensor(
                 out=fresh[g][:, c0:c1], in0=u[g][:, c0:c1], scalar=1.0, in1=cand[g][:, c0:c1],
                 op0=ALU.subtract, op1=ALU.mult,
             )
 
-        def finish(g, c0, c1):
-            nc.vector.tensor_tensor(out=y[g][:, c0:c1], in0=kept[g][:, c0:c1], in1=fresh[g][:, c0:c1], op=ALU.subtract)
+        def finish(engine, g, c0, c1):
+            engine.tensor_tensor(out=y[g][:, c0:c1], in0=kept[g][:, c0:c1], in1=fresh[g][:, c0:c1], op=ALU.subtract)
             for i in range(2):
                 lo, hi = max(c0, HALF * i), min(c1, HALF * (i + 1))
                 if lo < hi:
@@ -173,25 +177,40 @@ def tile_rows_pl_cell_gru_kernel(tc, h, wr, wu, wc, xr, xu, xc, hp, bc, out_0, o
             nc.sync.dma_start(out=out_0[M * g : M * (g + 1), c0:c1], in_=y[g][:, c0:c1])
 
         reset_gate(0)
+        reset_gate(1)
         quantize_w("wu")
         product(gate_bank, "wu", 0)
-        reset_gate(1)
         product(gate_bank, "wu", 1)
-        apply_reset(*UNITS[0])
-        update_gate(0)
-        for i, unit in enumerate(UNITS):
-            candidate(*unit)
-            if i > 0:
-                finish(*UNITS[i - 1])
-            if i + 2 < G:
-                reset_gate(i + 2)
-                product(gate_bank, "wu", i + 2)
-            if i + 1 < len(UNITS):
-                apply_reset(*UNITS[i + 1])
-            if i + 1 < G:
-                update_gate(i + 1)
-            mix_parts(*unit)
-        finish(*UNITS[-1])
+        apply_reset(0)
+        for g in range(G - 1):
+            if g == 0:
+                candidate_sum(nc.gpsimd, 0)
+            else:
+                finish(nc.gpsimd, g - 1, 0, N)
+            if g + 2 < G:
+                reset_gate(g + 2)
+                product(gate_bank, "wu", g + 2)
+            update_gate(g)
+            if g == 0:
+                candidate(0)
+            if g + 2 == G:
+                update_gate(g + 1)
+            apply_reset(g + 1)
+            candidate_sum(nc.vector, g + 1)
+            candidate(g + 1)
+            kept_part(g)
+            if g + 2 < G:
+                fresh_part(g, 0, N)
+        kept_part(3)
+        fresh_part(2, 0, HALF)
+        fresh_part(3, 0, HALF)
+        finish(nc.vector, 2, 0, HALF)
+        finish(nc.vector, 3, 0, HALF)
+        fresh_part(2, HALF, N)
+        fresh_part(3, HALF, N)
+        finish(nc.vector, 2, HALF, N)
+        finish(nc.vector, 3, HALF, HALF + 128)
+        finish(nc.vector, 3, HALF + 128, N)
 
         y_bf = [tile("y_bf%d" % i, [P, PACK * HALF], BF16) for i in range(2)]
         y_codes = tile("y_codes", [P, N], U32)

@@ -19,6 +19,8 @@ PACK = 4
 ROWS = D // PACK
 HALF = N // 2
 H_SPLIT = 416
+EARLY, LATE = 256, 384
+ORDER = (0, 2, 1, 3)
 
 
 def interleave(copy, grouped, raw, c0, c1, at):
@@ -38,8 +40,8 @@ def tile_rows_pl_cell_gru_kernel(tc, h, wr, wu, wc, xr, xu, xc, hp, bc, out_0, o
         def tile(name, shape, dtype):
             return sb.tile(shape, dtype, name=name, align_bytes=64)
 
-        def per_group(name):
-            return [tile("%s%d" % (name, g), [P, N], F32) for g in range(G)]
+        def per_group(name, width=N, dtype=F32):
+            return [tile("%s%d" % (name, i), [P, width], dtype) for i in range(G)]
 
         def quantize(codes, scales, grouped, c0, c1, at):
             nc.vector.quantize_mx(
@@ -51,31 +53,40 @@ def tile_rows_pl_cell_gru_kernel(tc, h, wr, wu, wc, xr, xu, xc, hp, bc, out_0, o
         h_raw = tile("h_raw", [P, PACK, N], F32)
         w_raw = {name: tile(name + "_raw", [P, PACK, M], F32) for name in ("wr", "wc", "wu")}
         w_src = {"wr": wr, "wc": wc, "wu": wu}
-        x_src = {"xr": xr, "xu": xu, "xc": xc, "hp": hp}
+        x_src = {"xr": xr, "xu": xu, "xc": xc}
         x_sb = {name: per_group(name) for name in x_src}
+        hp_sb = per_group("hp", LATE)
+        hp_late = tile("hp_late", [P, PACK, N - LATE], F32)
 
         def load_w(name):
             nc.sync.dma_start(out=w_raw[name][:], in_=w_src[name].rearrange("g (p j) m -> (g p) j m", j=PACK))
 
-        def load_x(name, g):
-            nc.sync.dma_start(out=x_sb[name][g][:], in_=x_src[name][g])
+        def load_x(name, i):
+            nc.sync.dma_start(out=x_sb[name][i][:], in_=x_src[name][ORDER[i]])
+
+        def load_hp(i):
+            nc.sync.dma_start(out=hp_sb[i][:], in_=hp[ORDER[i], :, 0:LATE])
 
         nc.sync.dma_start(out=h_raw[:], in_=h.rearrange("g (p j) n -> (g p) j n", j=PACK))
         load_w("wr")
         load_w("wc")
         load_x("xr", 0)
-        load_x("xr", 1)
         load_w("wu")
+        load_x("xr", 1)
         load_x("xc", 0)
-        for g in range(G - 1):
-            if g + 2 < G:
-                load_x("xr", g + 2)
-            load_x("xu", g)
-            if g + 2 == G:
-                load_x("xu", g + 1)
-            load_x("xc", g + 1)
-            load_x("hp", g)
-        load_x("hp", G - 1)
+        load_x("xr", 2)
+        load_x("xu", 0)
+        load_x("xc", 1)
+        load_hp(0)
+        load_x("xr", 3)
+        load_x("xu", 1)
+        load_x("xc", 2)
+        load_x("xu", 2)
+        load_x("xu", 3)
+        load_x("xc", 3)
+        for i in range(1, G):
+            load_hp(i)
+        nc.sync.dma_start(out=hp_late[:], in_=hp.rearrange("g (p x) n -> (g p) x n", x=PACK)[:, :, LATE:N])
 
         bias_rows = tile("bias_rows", [P, P], F32)
         bias_cols = tile("bias_cols", [P, P], F32)
@@ -100,7 +111,6 @@ def tile_rows_pl_cell_gru_kernel(tc, h, wr, wu, wc, xr, xu, xc, hp, bc, out_0, o
         def quantize_w(name):
             quantize(w_codes[name], w_scales[name], w_bf[name], 0, M, 0)
 
-        nc.vector.transpose(out=bias_cols[:], in_=bias_rows[:])
         interleave(nc.scalar.copy, h_bf[1], h_raw, H_SPLIT, N, H_SPLIT - HALF)
         interleave(nc.scalar.copy, w_bf["wr"], w_raw["wr"], 0, M, 0)
         interleave(nc.scalar.copy, w_bf["wc"], w_raw["wc"], 0, M, 0)
@@ -114,8 +124,11 @@ def tile_rows_pl_cell_gru_kernel(tc, h, wr, wu, wc, xr, xu, xc, hp, bc, out_0, o
         gate_bank = [ps.tile([P, N], F32, name="gate_bank%d" % g) for g in range(G)]
         cand_bank = [ps.tile([P, N], F32, name="cand_bank%d" % g) for g in range(G)]
 
+        def head_rows(i):
+            return slice(ROWS * ORDER[i], ROWS * (ORDER[i] + 1))
+
         def product(bank, name, g):
-            rows = slice(ROWS * g, ROWS * (g + 1))
+            rows = head_rows(g)
             nc.tensor.matmul_mx(
                 out=bank[g][:],
                 lhsT=w_codes[name][rows, :].bitcast(FP8X4),
@@ -126,106 +139,165 @@ def tile_rows_pl_cell_gru_kernel(tc, h, wr, wu, wc, xr, xu, xc, hp, bc, out_0, o
                 stop=True,
             )
 
-        for g in range(G):
-            product(gate_bank, "wr", g)
+        product(gate_bank, "wr", 0)
+        product(gate_bank, "wr", 1)
         quantize_w("wc")
-        for g in range(G):
-            product(cand_bank, "wc", g)
+        nc.vector.transpose(out=bias_cols[:], in_=bias_rows[:])
+        product(cand_bank, "wc", 0)
+        product(gate_bank, "wr", 2)
 
-        r_sum, r, u_sum, u = per_group("r_sum"), per_group("r"), per_group("u_sum"), per_group("u")
-        gated, c_sum, cand = per_group("gated"), per_group("c_sum"), per_group("cand")
-        kept, fresh, y = per_group("kept"), per_group("fresh"), per_group("y")
-        moved = [tile("moved%d" % i, [P, PACK, HALF], F32) for i in range(2)]
+        r_sum, r, u_sum = per_group("r_sum"), per_group("r"), per_group("u_sum")
+        gated, c_sum = per_group("gated"), per_group("c_sum")
+        u_cand = per_group("u_cand", 2 * N)
+        u = [t[:, 0:N] for t in u_cand]
+        cand = [t[:, N : 2 * N] for t in u_cand]
+        kept, fresh, y = per_group("kept", LATE), per_group("fresh", LATE), per_group("y", LATE)
+        y_round = per_group("y_round", EARLY, BF16)
+        parts = [(0, EARLY), (EARLY, LATE)]
+        moved_early = tile("moved_early", [P, PACK, EARLY], BF16)
+        moved_mid = tile("moved_mid", [P, PACK, LATE - EARLY], F32)
+        late = tile("late", [P, PACK, 2, N - LATE], F32)
 
-        def reset_gate(g):
-            nc.vector.tensor_tensor(out=r_sum[g][:], in0=gate_bank[g][:], in1=x_sb["xr"][g][:], op=ALU.add)
-            nc.scalar.activation(out=r[g][:], in_=r_sum[g][:], func=ACT.Sigmoid)
+        def reset_gate(i):
+            nc.vector.tensor_tensor(out=r_sum[i][:], in0=gate_bank[i][:], in1=x_sb["xr"][i][:], op=ALU.add)
+            nc.scalar.activation(out=r[i][:], in_=r_sum[i][:], func=ACT.Sigmoid)
 
-        def update_gate(g):
-            nc.vector.tensor_tensor(out=u_sum[g][:], in0=gate_bank[g][:], in1=x_sb["xu"][g][:], op=ALU.add)
-            nc.scalar.activation(out=u[g][:], in_=u_sum[g][:], func=ACT.Sigmoid)
+        def update_gate(i):
+            nc.vector.tensor_tensor(out=u_sum[i][:], in0=gate_bank[i][:], in1=x_sb["xu"][i][:], op=ALU.add)
+            nc.scalar.activation(out=u[i], in_=u_sum[i][:], func=ACT.Sigmoid)
 
-        def apply_reset(g):
+        def apply_reset(i):
             nc.vector.scalar_tensor_tensor(
-                out=gated[g][:], in0=cand_bank[g][:], scalar=bias_cols[:, 32 * g : 32 * g + 1],
-                in1=r[g][:], op0=ALU.add, op1=ALU.mult,
+                out=gated[i][:], in0=cand_bank[i][:], scalar=bias_cols[:, 32 * ORDER[i] : 32 * ORDER[i] + 1],
+                in1=r[i][:], op0=ALU.add, op1=ALU.mult,
             )
 
-        def candidate_sum(engine, g):
-            engine.tensor_tensor(out=c_sum[g][:], in0=gated[g][:], in1=x_sb["xc"][g][:], op=ALU.add)
+        def candidate_sum(engine, i):
+            engine.tensor_tensor(out=c_sum[i][:], in0=gated[i][:], in1=x_sb["xc"][i][:], op=ALU.add)
 
-        def candidate(g):
-            nc.scalar.activation(out=cand[g][:], in_=c_sum[g][:], func=ACT.Tanh)
+        def candidate(i):
+            nc.scalar.activation(out=cand[i], in_=c_sum[i][:], func=ACT.Tanh)
 
-        def kept_part(g):
-            nc.vector.tensor_tensor(out=kept[g][:], in0=u[g][:], in1=x_sb["hp"][g][:], op=ALU.mult)
+        def kept_part(out, u_part, hp_part):
+            nc.vector.tensor_tensor(out=out, in0=u_part, in1=hp_part, op=ALU.mult)
 
-        def fresh_part(g, c0, c1):
+        def fresh_part(out, u_part, cand_part):
             nc.vector.scalar_tensor_tensor(
-                out=fresh[g][:, c0:c1], in0=u[g][:, c0:c1], scalar=1.0, in1=cand[g][:, c0:c1],
-                op0=ALU.subtract, op1=ALU.mult,
+                out=out, in0=u_part, scalar=1.0, in1=cand_part, op0=ALU.subtract, op1=ALU.mult
             )
 
-        def finish(engine, g, c0, c1):
-            engine.tensor_tensor(out=y[g][:, c0:c1], in0=kept[g][:, c0:c1], in1=fresh[g][:, c0:c1], op=ALU.subtract)
-            for i in range(2):
-                lo, hi = max(c0, HALF * i), min(c1, HALF * (i + 1))
-                if lo < hi:
-                    nc.sync.dma_start(
-                        out=moved[i][ROWS * g : ROWS * (g + 1), :, lo - HALF * i : hi - HALF * i], in_=y[g][:, lo:hi]
-                    )
-            nc.sync.dma_start(out=out_0[M * g : M * (g + 1), c0:c1], in_=y[g][:, c0:c1])
+        def keep(i, c0, c1):
+            kept_part(kept[i][:, c0:c1], u[i][:, c0:c1], hp_sb[i][:, c0:c1])
+
+        def renew(i, c0, c1):
+            fresh_part(fresh[i][:, c0:c1], u[i][:, c0:c1], cand[i][:, c0:c1])
+
+        def mix(engine, i, c0, c1):
+            engine.tensor_tensor(out=y[i][:, c0:c1], in0=kept[i][:, c0:c1], in1=fresh[i][:, c0:c1], op=ALU.subtract)
+
+        def move_early(i):
+            nc.scalar.copy(out=y_round[i][:], in_=y[i][:, 0:EARLY])
+            nc.sync.dma_start(out=moved_early[head_rows(i), :, :], in_=y_round[i][:])
+
+        def move_mid(i):
+            nc.sync.dma_start(out=moved_mid[head_rows(i), :, :], in_=y[i][:, EARLY:LATE])
+
+        def move_late(i):
+            nc.sync.dma_start(
+                out=late[head_rows(i), :, :, :].rearrange("p x k n -> p (x k) n"),
+                in_=u_cand[i][:].rearrange("m (k n) -> m k n", k=2)[:, :, LATE:N],
+            )
+
+        def store(i):
+            nc.sync.dma_start(out=out_0[M * ORDER[i] : M * (ORDER[i] + 1), 0:LATE], in_=y[i][:])
 
         reset_gate(0)
         reset_gate(1)
         quantize_w("wu")
         product(gate_bank, "wu", 0)
+        product(cand_bank, "wc", 1)
+        product(gate_bank, "wr", 3)
         product(gate_bank, "wu", 1)
+        product(cand_bank, "wc", 2)
+        product(cand_bank, "wc", 3)
         apply_reset(0)
-        for g in range(G - 1):
-            if g == 0:
-                candidate_sum(nc.gpsimd, 0)
-            else:
-                finish(nc.gpsimd, g - 1, 0, N)
-            if g + 2 < G:
-                reset_gate(g + 2)
-                product(gate_bank, "wu", g + 2)
-            update_gate(g)
-            if g == 0:
-                candidate(0)
-            if g + 2 == G:
-                update_gate(g + 1)
-            apply_reset(g + 1)
-            candidate_sum(nc.vector, g + 1)
-            candidate(g + 1)
-            kept_part(g)
-            if g + 2 < G:
-                fresh_part(g, 0, N)
-        kept_part(3)
-        fresh_part(2, 0, HALF)
-        fresh_part(3, 0, HALF)
-        finish(nc.vector, 2, 0, HALF)
-        finish(nc.vector, 3, 0, HALF)
-        fresh_part(2, HALF, N)
-        fresh_part(3, HALF, N)
-        finish(nc.vector, 2, HALF, N)
-        finish(nc.vector, 3, HALF, HALF + 128)
-        finish(nc.vector, 3, HALF + 128, N)
 
-        y_bf = [tile("y_bf%d" % i, [P, PACK * HALF], BF16) for i in range(2)]
+        candidate_sum(nc.gpsimd, 0)
+        reset_gate(2)
+        product(gate_bank, "wu", 2)
+        update_gate(0)
+        candidate(0)
+        move_late(0)
+        apply_reset(1)
+
+        candidate_sum(nc.vector, 1)
+        candidate(1)
+        keep(0, 0, LATE)
+        renew(0, 0, LATE)
+
+        mix(nc.gpsimd, 0, 0, LATE)
+        reset_gate(3)
+        product(gate_bank, "wu", 3)
+        update_gate(1)
+        move_late(1)
+        move_mid(0)
+        move_early(0)
+        apply_reset(2)
+        candidate_sum(nc.gpsimd, 2)
+        update_gate(2)
+        candidate(2)
+        move_late(2)
+        apply_reset(3)
+        update_gate(3)
+
+        candidate_sum(nc.vector, 3)
+        candidate(3)
+        move_late(3)
+        store(0)
+        keep(1, 0, LATE)
+        renew(1, 0, LATE)
+        keep(2, 0, EARLY)
+        mix(nc.vector, 1, 0, LATE)
+        move_early(1)
+        move_mid(1)
+        keep(3, 0, EARLY)
+        for i in (2, 3):
+            renew(i, 0, EARLY)
+        for i in (2, 3):
+            mix(nc.vector, i, 0, EARLY)
+            move_early(i)
+        store(1)
+        for step in (keep, renew):
+            for i in (2, 3):
+                step(i, EARLY, LATE)
+        for i in (2, 3):
+            mix(nc.vector, i, EARLY, LATE)
+            move_mid(i)
+        for i in (2, 3):
+            store(i)
+
+        kept_late = tile("kept_late", [P, PACK, N - LATE], F32)
+        fresh_late = tile("fresh_late", [P, PACK, N - LATE], F32)
+        y_late = tile("y_late", [P, PACK, N - LATE], F32)
+        fresh_part(fresh_late[:], late[:, :, 0, :], late[:, :, 1, :])
+        kept_part(kept_late[:], late[:, :, 0, :], hp_late[:])
+        nc.vector.tensor_tensor(out=y_late[:], in0=kept_late[:], in1=fresh_late[:], op=ALU.subtract)
+        nc.sync.dma_start(out=out_0.rearrange("(q x) n -> q x n", x=PACK)[:, :, LATE:N], in_=y_late[:])
+
+        spans = parts + [(LATE, N)]
+        y_bf = [tile("y_bf%d" % k, [P, PACK * (c1 - c0)], BF16) for k, (c0, c1) in enumerate(spans)]
         y_codes = tile("y_codes", [P, N], U32)
         y_scales = tile("y_scales", [P, N], U8)
         words = out_1.rearrange("s p n x -> (s p) (n x)").bitcast(I32)
         scale_rows = out_2.rearrange("s f n -> (s f) n").bitcast(I32)
 
-        interleave(nc.vector.tensor_copy, y_bf[0], moved[0], 0, HALF, 0)
-        quantize(y_codes, y_scales, y_bf[0], 0, HALF, 0)
-        nc.sync.dma_start(out=words[:, 0:HALF], in_=y_codes[:, 0:HALF].bitcast(I32))
-        interleave(nc.vector.tensor_copy, y_bf[1], moved[1], 0, 128, 0)
-        interleave(nc.vector.tensor_copy, y_bf[1], moved[1], 128, HALF, 128)
-        quantize(y_codes, y_scales, y_bf[1], HALF, HALF + 128, 0)
-        quantize(y_codes, y_scales, y_bf[1], HALF + 128, N, 128)
-        nc.sync.dma_start(out=words[:, HALF:N], in_=y_codes[:, HALF:N].bitcast(I32))
+        interleave(nc.scalar.copy, y_bf[0], moved_early, 0, EARLY, 0)
+        interleave(nc.vector.tensor_copy, y_bf[2], y_late, 0, N - LATE, 0)
+        interleave(nc.vector.tensor_copy, y_bf[1], moved_mid, 0, LATE - EARLY, 0)
+        for k in (2, 1, 0):
+            c0, c1 = spans[k]
+            quantize(y_codes, y_scales, y_bf[k], c0, c1, 0)
+            nc.sync.dma_start(out=words[:, c0:c1], in_=y_codes[:, c0:c1].bitcast(I32))
         for q in range(4):
             queue = nc.scalar if q < 2 else nc.sync
             queue.dma_start(out=scale_rows[4 * q : 4 * q + 4, :], in_=y_scales[32 * q : 32 * q + 4, :].bitcast(I32))

@@ -17,16 +17,18 @@ ACT = mybir.ActivationFunctionType
 P = 128
 PACK = 4
 ROWS = D // PACK
+QUAD = 32
+RUN = 4
 HALF = N // 2
-H_SPLIT = 416
-EARLY, LATE = 256, 384
+H_SPLIT = 384
+EARLY = 256
+LATE = 384
 ORDER = (0, 2, 1, 3)
 
 
 def interleave(copy, grouped, raw, c0, c1, at):
-    width = c1 - c0
-    dst = grouped[:, PACK * at : PACK * (at + width)].rearrange("p (c i j) -> p c j i", i=4, j=PACK)
-    src = raw[:, :, c0:c1].rearrange("p j (c i) -> p c j i", i=4)
+    dst = grouped[:, PACK * at : PACK * (at + c1 - c0)].rearrange("p (c i j) -> p c j i", i=RUN, j=PACK)
+    src = raw[:, :, c0:c1].rearrange("p j (c i) -> p c j i", i=RUN)
     copy(out=dst, in_=src)
 
 
@@ -40,7 +42,7 @@ def tile_rows_pl_cell_gru_kernel(tc, h, wr, wu, wc, xr, xu, xc, hp, bc, out_0, o
         def tile(name, shape, dtype):
             return sb.tile(shape, dtype, name=name, align_bytes=64)
 
-        def per_group(name, width=N, dtype=F32):
+        def per_turn(name, width=N, dtype=F32):
             return [tile("%s%d" % (name, i), [P, width], dtype) for i in range(G)]
 
         def quantize(codes, scales, grouped, c0, c1, at):
@@ -54,12 +56,9 @@ def tile_rows_pl_cell_gru_kernel(tc, h, wr, wu, wc, xr, xu, xc, hp, bc, out_0, o
         w_raw = {name: tile(name + "_raw", [P, PACK, M], F32) for name in ("wr", "wc", "wu")}
         w_src = {"wr": wr, "wc": wc, "wu": wu}
         x_src = {"xr": xr, "xu": xu, "xc": xc}
-        x_sb = {name: per_group(name) for name in x_src}
-        hp_sb = per_group("hp", LATE)
+        x_sb = {name: per_turn(name) for name in x_src}
+        hp_sb = per_turn("hp", LATE)
         hp_late = tile("hp_late", [P, PACK, N - LATE], F32)
-
-        def load_w(name):
-            nc.sync.dma_start(out=w_raw[name][:], in_=w_src[name].rearrange("g (p j) m -> (g p) j m", j=PACK))
 
         def load_x(name, i):
             nc.sync.dma_start(out=x_sb[name][i][:], in_=x_src[name][ORDER[i]])
@@ -68,14 +67,13 @@ def tile_rows_pl_cell_gru_kernel(tc, h, wr, wu, wc, xr, xu, xc, hp, bc, out_0, o
             nc.sync.dma_start(out=hp_sb[i][:], in_=hp[ORDER[i], :, 0:LATE])
 
         nc.sync.dma_start(out=h_raw[:], in_=h.rearrange("g (p j) n -> (g p) j n", j=PACK))
-        load_w("wr")
-        load_w("wc")
+        for name in w_raw:
+            nc.sync.dma_start(out=w_raw[name][:], in_=w_src[name].rearrange("g (p j) m -> (g p) j m", j=PACK))
         load_x("xr", 0)
-        load_w("wu")
         load_x("xr", 1)
         load_x("xc", 0)
-        load_x("xr", 2)
         load_x("xu", 0)
+        load_x("xr", 2)
         load_x("xc", 1)
         load_hp(0)
         load_x("xr", 3)
@@ -92,47 +90,41 @@ def tile_rows_pl_cell_gru_kernel(tc, h, wr, wu, wc, xr, xu, xc, hp, bc, out_0, o
         bias_cols = tile("bias_cols", [P, P], F32)
         nc.vector.memset(bias_rows[:], 0.0)
         nc.scalar.dma_start(
-            out=bias_rows[0:P:32, :].rearrange("q (g i) -> q g i", g=G),
-            in_=bc.rearrange("g (q i) o -> q g (i o)", i=32),
+            out=bias_rows[0:P:QUAD, :].rearrange("q (g i) -> q g i", g=G),
+            in_=bc.rearrange("g (q i) o -> q g (i o)", i=QUAD),
         )
 
-        warm_in = tile("warm_in", [P, 1], F32)
-        warm_out = tile("warm_out", [P, 1], F32)
-        nc.vector.memset(warm_in[:], 0.0)
-        nc.scalar.activation(out=warm_out[:], in_=warm_in[:], func=ACT.Sigmoid)
-
-        w_bf = {name: tile(name + "_bf", [P, PACK * M], BF16) for name in w_raw}
-        w_codes = {name: tile(name + "_codes", [P, M], U32) for name in w_raw}
-        w_scales = {name: tile(name + "_scales", [P, M], U8) for name in w_raw}
-        h_bf = [tile("h_bf%d" % i, [P, PACK * HALF], BF16) for i in range(2)]
+        wr_bf = tile("wr_bf", [P, PACK * M], BF16)
+        wcu_bf = tile("wcu_bf", [P, 2 * PACK * M], BF16)
+        w_codes = tile("w_codes", [P, 3 * M], U32)
+        w_scales = tile("w_scales", [P, 3 * M], U8)
+        w_cols = {"wr": slice(0, M), "wc": slice(M, 2 * M), "wu": slice(2 * M, 3 * M)}
+        h_bf = [tile("h_bf%d" % k, [P, PACK * HALF], BF16) for k in range(2)]
         h_codes = tile("h_codes", [P, N], U32)
         h_scales = tile("h_scales", [P, N], U8)
 
-        def quantize_w(name):
-            quantize(w_codes[name], w_scales[name], w_bf[name], 0, M, 0)
-
         interleave(nc.scalar.copy, h_bf[1], h_raw, H_SPLIT, N, H_SPLIT - HALF)
-        interleave(nc.scalar.copy, w_bf["wr"], w_raw["wr"], 0, M, 0)
-        interleave(nc.scalar.copy, w_bf["wc"], w_raw["wc"], 0, M, 0)
-        interleave(nc.scalar.copy, w_bf["wu"], w_raw["wu"], 0, M, 0)
+        interleave(nc.scalar.copy, wr_bf, w_raw["wr"], 0, M, 0)
         interleave(nc.vector.tensor_copy, h_bf[0], h_raw, 0, HALF, 0)
         interleave(nc.vector.tensor_copy, h_bf[1], h_raw, HALF, H_SPLIT, 0)
         quantize(h_codes, h_scales, h_bf[0], 0, HALF, 0)
         quantize(h_codes, h_scales, h_bf[1], HALF, N, 0)
-        quantize_w("wr")
+        quantize(w_codes, w_scales, wr_bf, 0, M, 0)
+        interleave(nc.vector.tensor_copy, wcu_bf, w_raw["wc"], 0, M, 0)
+        interleave(nc.vector.tensor_copy, wcu_bf, w_raw["wu"], 0, M, M)
 
-        gate_bank = [ps.tile([P, N], F32, name="gate_bank%d" % g) for g in range(G)]
-        cand_bank = [ps.tile([P, N], F32, name="cand_bank%d" % g) for g in range(G)]
+        gate_bank = [ps.tile([P, N], F32, name="gate_bank%d" % i) for i in range(G)]
+        cand_bank = [ps.tile([P, N], F32, name="cand_bank%d" % i) for i in range(G)]
 
         def head_rows(i):
             return slice(ROWS * ORDER[i], ROWS * (ORDER[i] + 1))
 
-        def product(bank, name, g):
-            rows = head_rows(g)
+        def product(bank, name, i):
+            rows = head_rows(i)
             nc.tensor.matmul_mx(
-                out=bank[g][:],
-                lhsT=w_codes[name][rows, :].bitcast(FP8X4),
-                lhsT_scale=w_scales[name][rows, :],
+                out=bank[i][:],
+                lhsT=w_codes[rows, w_cols[name]].bitcast(FP8X4),
+                lhsT_scale=w_scales[rows, w_cols[name]],
                 rhs=h_codes[rows, :].bitcast(FP8X4),
                 rhs_scale=h_scales[rows, :],
                 start=True,
@@ -141,22 +133,22 @@ def tile_rows_pl_cell_gru_kernel(tc, h, wr, wu, wc, xr, xu, xc, hp, bc, out_0, o
 
         product(gate_bank, "wr", 0)
         product(gate_bank, "wr", 1)
-        quantize_w("wc")
+        quantize(w_codes, w_scales, wcu_bf, M, 2 * M, 0)
         nc.vector.transpose(out=bias_cols[:], in_=bias_rows[:])
         product(cand_bank, "wc", 0)
+        product(cand_bank, "wc", 1)
         product(gate_bank, "wr", 2)
 
-        r_sum, r, u_sum = per_group("r_sum"), per_group("r"), per_group("u_sum")
-        gated, c_sum = per_group("gated"), per_group("c_sum")
-        u_cand = per_group("u_cand", 2 * N)
+        r_sum, r, u_sum = per_turn("r_sum"), per_turn("r"), per_turn("u_sum")
+        gated, c_sum = per_turn("gated"), per_turn("c_sum")
+        u_cand = per_turn("u_cand", 2 * N)
         u = [t[:, 0:N] for t in u_cand]
         cand = [t[:, N : 2 * N] for t in u_cand]
-        kept, fresh, y = per_group("kept", LATE), per_group("fresh", LATE), per_group("y", LATE)
-        y_round = per_group("y_round", EARLY, BF16)
-        parts = [(0, EARLY), (EARLY, LATE)]
+        kept, fresh, y = per_turn("kept", LATE), per_turn("fresh", LATE), per_turn("y", LATE)
+        y_round = per_turn("y_round", LATE, BF16)
         moved_early = tile("moved_early", [P, PACK, EARLY], BF16)
-        moved_mid = tile("moved_mid", [P, PACK, LATE - EARLY], F32)
-        late = tile("late", [P, PACK, 2, N - LATE], F32)
+        moved_mid = tile("moved_mid", [P, PACK, LATE - EARLY], BF16)
+        u_cand_late = tile("u_cand_late", [P, PACK, 2, N - LATE], F32)
 
         def reset_gate(i):
             nc.vector.tensor_tensor(out=r_sum[i][:], in0=gate_bank[i][:], in1=x_sb["xr"][i][:], op=ALU.add)
@@ -167,8 +159,9 @@ def tile_rows_pl_cell_gru_kernel(tc, h, wr, wu, wc, xr, xu, xc, hp, bc, out_0, o
             nc.scalar.activation(out=u[i], in_=u_sum[i][:], func=ACT.Sigmoid)
 
         def apply_reset(i):
+            column = QUAD * ORDER[i]
             nc.vector.scalar_tensor_tensor(
-                out=gated[i][:], in0=cand_bank[i][:], scalar=bias_cols[:, 32 * ORDER[i] : 32 * ORDER[i] + 1],
+                out=gated[i][:], in0=cand_bank[i][:], scalar=bias_cols[:, column : column + 1],
                 in1=r[i][:], op0=ALU.add, op1=ALU.mult,
             )
 
@@ -195,16 +188,18 @@ def tile_rows_pl_cell_gru_kernel(tc, h, wr, wu, wc, xr, xu, xc, hp, bc, out_0, o
         def mix(engine, i, c0, c1):
             engine.tensor_tensor(out=y[i][:, c0:c1], in0=kept[i][:, c0:c1], in1=fresh[i][:, c0:c1], op=ALU.subtract)
 
+        def round_y(i, c0, c1):
+            nc.scalar.copy(out=y_round[i][:, c0:c1], in_=y[i][:, c0:c1])
+
         def move_early(i):
-            nc.scalar.copy(out=y_round[i][:], in_=y[i][:, 0:EARLY])
-            nc.sync.dma_start(out=moved_early[head_rows(i), :, :], in_=y_round[i][:])
+            nc.sync.dma_start(out=moved_early[head_rows(i), :, :], in_=y_round[i][:, 0:EARLY])
 
         def move_mid(i):
-            nc.sync.dma_start(out=moved_mid[head_rows(i), :, :], in_=y[i][:, EARLY:LATE])
+            nc.sync.dma_start(out=moved_mid[head_rows(i), :, :], in_=y_round[i][:, EARLY:LATE])
 
         def move_late(i):
             nc.sync.dma_start(
-                out=late[head_rows(i), :, :, :].rearrange("p x k n -> p (x k) n"),
+                out=u_cand_late[head_rows(i), :, :, :].rearrange("p x k n -> p (x k) n"),
                 in_=u_cand[i][:].rearrange("m (k n) -> m k n", k=2)[:, :, LATE:N],
             )
 
@@ -213,9 +208,8 @@ def tile_rows_pl_cell_gru_kernel(tc, h, wr, wu, wc, xr, xu, xc, hp, bc, out_0, o
 
         reset_gate(0)
         reset_gate(1)
-        quantize_w("wu")
+        quantize(w_codes, w_scales, wcu_bf, 2 * M, 3 * M, M)
         product(gate_bank, "wu", 0)
-        product(cand_bank, "wc", 1)
         product(gate_bank, "wr", 3)
         product(gate_bank, "wu", 1)
         product(cand_bank, "wc", 2)
@@ -223,12 +217,12 @@ def tile_rows_pl_cell_gru_kernel(tc, h, wr, wu, wc, xr, xu, xc, hp, bc, out_0, o
         apply_reset(0)
 
         candidate_sum(nc.gpsimd, 0)
-        reset_gate(2)
-        product(gate_bank, "wu", 2)
+        apply_reset(1)
         update_gate(0)
         candidate(0)
         move_late(0)
-        apply_reset(1)
+        reset_gate(2)
+        product(gate_bank, "wu", 2)
 
         candidate_sum(nc.vector, 1)
         candidate(1)
@@ -240,8 +234,9 @@ def tile_rows_pl_cell_gru_kernel(tc, h, wr, wu, wc, xr, xu, xc, hp, bc, out_0, o
         product(gate_bank, "wu", 3)
         update_gate(1)
         move_late(1)
-        move_mid(0)
+        round_y(0, 0, LATE)
         move_early(0)
+        move_mid(0)
         apply_reset(2)
         candidate_sum(nc.gpsimd, 2)
         update_gate(2)
@@ -258,46 +253,61 @@ def tile_rows_pl_cell_gru_kernel(tc, h, wr, wu, wc, xr, xu, xc, hp, bc, out_0, o
         renew(1, 0, LATE)
         keep(2, 0, EARLY)
         mix(nc.vector, 1, 0, LATE)
+        round_y(1, 0, LATE)
         move_early(1)
         move_mid(1)
         keep(3, 0, EARLY)
-        for i in (2, 3):
+        last_turns = (G - 2, G - 1)
+        for i in last_turns:
             renew(i, 0, EARLY)
-        for i in (2, 3):
+        for i in last_turns:
             mix(nc.vector, i, 0, EARLY)
+            round_y(i, 0, EARLY)
             move_early(i)
         store(1)
         for step in (keep, renew):
-            for i in (2, 3):
+            for i in last_turns:
                 step(i, EARLY, LATE)
-        for i in (2, 3):
+        for i in last_turns:
             mix(nc.vector, i, EARLY, LATE)
+            round_y(i, EARLY, LATE)
             move_mid(i)
-        for i in (2, 3):
+        for i in last_turns:
             store(i)
 
         kept_late = tile("kept_late", [P, PACK, N - LATE], F32)
         fresh_late = tile("fresh_late", [P, PACK, N - LATE], F32)
         y_late = tile("y_late", [P, PACK, N - LATE], F32)
-        fresh_part(fresh_late[:], late[:, :, 0, :], late[:, :, 1, :])
-        kept_part(kept_late[:], late[:, :, 0, :], hp_late[:])
-        nc.vector.tensor_tensor(out=y_late[:], in0=kept_late[:], in1=fresh_late[:], op=ALU.subtract)
+        u_late, cand_late = u_cand_late[:, :, 0, :], u_cand_late[:, :, 1, :]
+        halves = [slice(0, (N - LATE) // 2), slice((N - LATE) // 2, N - LATE)]
+        fresh_part(fresh_late[:], u_late, cand_late)
+        for cols in halves:
+            kept_part(kept_late[:, :, cols], u_late[:, :, cols], hp_late[:, :, cols])
+        for cols in halves:
+            nc.vector.tensor_tensor(
+                out=y_late[:, :, cols], in0=kept_late[:, :, cols], in1=fresh_late[:, :, cols], op=ALU.subtract
+            )
         nc.sync.dma_start(out=out_0.rearrange("(q x) n -> q x n", x=PACK)[:, :, LATE:N], in_=y_late[:])
 
-        spans = parts + [(LATE, N)]
-        y_bf = [tile("y_bf%d" % k, [P, PACK * (c1 - c0)], BF16) for k, (c0, c1) in enumerate(spans)]
+        early_bf = tile("early_bf", [P, PACK * EARLY], BF16)
+        mid_bf = tile("mid_bf", [P, PACK * (LATE - EARLY)], BF16)
+        late_bf = tile("late_bf", [P, PACK * (N - LATE)], BF16)
         y_codes = tile("y_codes", [P, N], U32)
         y_scales = tile("y_scales", [P, N], U8)
         words = out_1.rearrange("s p n x -> (s p) (n x)").bitcast(I32)
         scale_rows = out_2.rearrange("s f n -> (s f) n").bitcast(I32)
 
-        interleave(nc.scalar.copy, y_bf[0], moved_early, 0, EARLY, 0)
-        interleave(nc.vector.tensor_copy, y_bf[2], y_late, 0, N - LATE, 0)
-        interleave(nc.vector.tensor_copy, y_bf[1], moved_mid, 0, LATE - EARLY, 0)
-        for k in (2, 1, 0):
-            c0, c1 = spans[k]
-            quantize(y_codes, y_scales, y_bf[k], c0, c1, 0)
+        interleave(nc.scalar.copy, early_bf, moved_early, 0, EARLY, 0)
+        for cols in halves:
+            interleave(nc.vector.tensor_copy, late_bf, y_late, cols.start, cols.stop, cols.start)
+        interleave(nc.vector.tensor_copy, mid_bf, moved_mid, 0, LATE - EARLY, 0)
+        for grouped, c0, c1 in ((late_bf, LATE, N), (mid_bf, EARLY, LATE), (early_bf, 0, EARLY)):
+            quantize(y_codes, y_scales, grouped, c0, c1, 0)
             nc.sync.dma_start(out=words[:, c0:c1], in_=y_codes[:, c0:c1].bitcast(I32))
-        for q in range(4):
+        blocks = QUAD * PACK // 32
+        for q in range(P // QUAD):
             queue = nc.scalar if q < 2 else nc.sync
-            queue.dma_start(out=scale_rows[4 * q : 4 * q + 4, :], in_=y_scales[32 * q : 32 * q + 4, :].bitcast(I32))
+            queue.dma_start(
+                out=scale_rows[blocks * q : blocks * (q + 1), :],
+                in_=y_scales[QUAD * q : QUAD * q + blocks, :].bitcast(I32),
+            )

@@ -82,9 +82,8 @@ def tile_rows_pl_cell_gru_kernel(tc, h, wr, wu, wc, xr, xu, xc, hp, bc, out_0, o
         load_x("xu", 2)
         load_x("xu", 3)
         load_x("xc", 3)
-        for i in range(1, G):
+        for i in range(1, G - 1):
             load_hp(i)
-        nc.sync.dma_start(out=hp_late[:], in_=hp.rearrange("g (p x) n -> (g p) x n", x=PACK)[:, :, LATE:N])
 
         bias_rows = tile("bias_rows", [P, P], F32)
         bias_cols = tile("bias_cols", [P, P], F32)
@@ -165,8 +164,8 @@ def tile_rows_pl_cell_gru_kernel(tc, h, wr, wu, wc, xr, xu, xc, hp, bc, out_0, o
                 in1=r[i][:], op0=ALU.add, op1=ALU.mult,
             )
 
-        def candidate_sum(engine, i):
-            engine.tensor_tensor(out=c_sum[i][:], in0=gated[i][:], in1=x_sb["xc"][i][:], op=ALU.add)
+        def candidate_sum(engine, i, c0=0, c1=N):
+            engine.tensor_tensor(out=c_sum[i][:, c0:c1], in0=gated[i][:, c0:c1], in1=x_sb["xc"][i][:, c0:c1], op=ALU.add)
 
         def candidate(i):
             nc.scalar.activation(out=cand[i], in_=c_sum[i][:], func=ACT.Tanh)
@@ -203,8 +202,8 @@ def tile_rows_pl_cell_gru_kernel(tc, h, wr, wu, wc, xr, xu, xc, hp, bc, out_0, o
                 in_=u_cand[i][:].rearrange("m (k n) -> m k n", k=2)[:, :, LATE:N],
             )
 
-        def store(i):
-            nc.sync.dma_start(out=out_0[M * ORDER[i] : M * (ORDER[i] + 1), 0:LATE], in_=y[i][:])
+        def store(i, queue=nc.sync):
+            queue.dma_start(out=out_0[M * ORDER[i] : M * (ORDER[i] + 1), 0:LATE], in_=y[i][:])
 
         reset_gate(0)
         reset_gate(1)
@@ -224,17 +223,20 @@ def tile_rows_pl_cell_gru_kernel(tc, h, wr, wu, wc, xr, xu, xc, hp, bc, out_0, o
         reset_gate(2)
         product(gate_bank, "wu", 2)
 
-        candidate_sum(nc.vector, 1)
-        candidate(1)
+        candidate_sum(nc.vector, 1, 0, 320)
         keep(0, 0, LATE)
         renew(0, 0, LATE)
 
         mix(nc.gpsimd, 0, 0, LATE)
+        candidate_sum(nc.gpsimd, 1, 320, N)
         reset_gate(3)
         product(gate_bank, "wu", 3)
         update_gate(1)
+        candidate(1)
         move_late(1)
         round_y(0, 0, LATE)
+        nc.scalar.dma_start(out=hp_sb[3][:], in_=hp[ORDER[3], :, 0:LATE])
+        nc.scalar.dma_start(out=hp_late[:], in_=hp.rearrange("g (p x) n -> (g p) x n", x=PACK)[:, :, LATE:N])
         move_early(0)
         move_mid(0)
         apply_reset(2)
@@ -248,7 +250,7 @@ def tile_rows_pl_cell_gru_kernel(tc, h, wr, wu, wc, xr, xu, xc, hp, bc, out_0, o
         candidate_sum(nc.vector, 3)
         candidate(3)
         move_late(3)
-        store(0)
+        store(0, nc.scalar)
         keep(1, 0, LATE)
         renew(1, 0, LATE)
         keep(2, 0, EARLY)

from contextlib import ExitStack

import concourse.mybir as mybir

G, D, M, N = 4, 128, 128, 512
FLOPS = 3 * 2 * G * D * M * N

F32 = mybir.dt.float32
BF16 = mybir.dt.bfloat16
I32 = mybir.dt.int32
U32 = mybir.dt.uint32
U8 = mybir.dt.uint8
FP8X4 = mybir.dt.float8_e4m3fn_x4
ALU = mybir.AluOpType
ACT = mybir.ActivationFunctionType

P = 128
PACK = 4
ROWS = D // PACK
QUAD = 32
RUN = 4
HALF = N // 2
H_SPLIT = 384
EARLY = 256
LATE = 384
ORDER = (0, 2, 1, 3)


def interleave(copy, grouped, raw, c0, c1, at):
    dst = grouped[:, PACK * at : PACK * (at + c1 - c0)].rearrange("p (c i j) -> p c j i", i=RUN, j=PACK)
    src = raw[:, :, c0:c1].rearrange("p j (c i) -> p c j i", i=RUN)
    copy(out=dst, in_=src)


def tile_rows_pl_cell_gru_kernel(tc, h, wr, wu, wc, xr, xu, xc, hp, bc, out_0, out_1, out_2):
    nc = tc.nc
    with ExitStack() as ctx:
        sb = ctx.enter_context(tc.tile_pool(name="sb", bufs=1))
        ps = ctx.enter_context(tc.psum_pool(name="ps", bufs=1))
        ctx.enter_context(tc.manual_schedule())

        def tile(name, shape, dtype):
            return sb.tile(shape, dtype, name=name, align_bytes=64)

        def per_turn(name, width=N, dtype=F32):
            return [tile("%s%d" % (name, i), [P, width], dtype) for i in range(G)]

        def quantize(codes, scales, grouped, c0, c1, at):
            nc.vector.quantize_mx(
                out=codes[:, c0:c1].bitcast(FP8X4),
                scales=scales[:, c0:c1],
                in_=grouped[:, PACK * at : PACK * (at + c1 - c0)],
            )

        h_raw = tile("h_raw", [P, PACK, N], F32)
        w_raw = {name: tile(name + "_raw", [P, PACK, M], F32) for name in ("wr", "wc", "wu")}
        w_src = {"wr": wr, "wc": wc, "wu": wu}
        x_src = {"xr": xr, "xu": xu, "xc": xc}
        x_sb = {name: per_turn(name) for name in x_src}
        hp_sb = per_turn("hp", LATE)
        hp_late = tile("hp_late", [P, PACK, N - LATE], F32)

        def load_x(name, i):
            nc.sync.dma_start(out=x_sb[name][i][:], in_=x_src[name][ORDER[i]])

        def load_hp(i):
            nc.sync.dma_start(out=hp_sb[i][:], in_=hp[ORDER[i], :, 0:LATE])

        nc.sync.dma_start(out=h_raw[:], in_=h.rearrange("g (p j) n -> (g p) j n", j=PACK))
        for name in w_raw:
            nc.sync.dma_start(out=w_raw[name][:], in_=w_src[name].rearrange("g (p j) m -> (g p) j m", j=PACK))
        load_x("xr", 0)
        load_x("xr", 1)
        load_x("xc", 0)
        load_x("xu", 0)
        load_x("xr", 2)
        load_x("xc", 1)
        load_hp(0)
        load_x("xr", 3)
        load_x("xu", 1)
        load_x("xc", 2)
        load_x("xu", 2)
        load_x("xu", 3)
        load_x("xc", 3)
        for i in range(1, G - 1):
            load_hp(i)

        bias_rows = tile("bias_rows", [P, P], F32)
        bias_cols = tile("bias_cols", [P, P], F32)
        nc.vector.memset(bias_rows[:], 0.0)
        nc.scalar.dma_start(
            out=bias_rows[0:P:QUAD, :].rearrange("q (g i) -> q g i", g=G),
            in_=bc.rearrange("g (q i) o -> q g (i o)", i=QUAD),
        )

        wr_bf = tile("wr_bf", [P, PACK * M], BF16)
        wcu_bf = tile("wcu_bf", [P, 2 * PACK * M], BF16)
        w_codes = tile("w_codes", [P, 3 * M], U32)
        w_scales = tile("w_scales", [P, 3 * M], U8)
        w_cols = {"wr": slice(0, M), "wc": slice(M, 2 * M), "wu": slice(2 * M, 3 * M)}
        h_bf = [tile("h_bf%d" % k, [P, PACK * HALF], BF16) for k in range(2)]
        h_codes = tile("h_codes", [P, N], U32)
        h_scales = tile("h_scales", [P, N], U8)

        interleave(nc.scalar.copy, h_bf[1], h_raw, H_SPLIT, N, H_SPLIT - HALF)
        interleave(nc.scalar.copy, wr_bf, w_raw["wr"], 0, M, 0)
        interleave(nc.vector.tensor_copy, h_bf[0], h_raw, 0, HALF, 0)
        interleave(nc.vector.tensor_copy, h_bf[1], h_raw, HALF, H_SPLIT, 0)
        quantize(h_codes, h_scales, h_bf[0], 0, HALF, 0)
        quantize(h_codes, h_scales, h_bf[1], HALF, N, 0)
        quantize(w_codes, w_scales, wr_bf, 0, M, 0)
        interleave(nc.vector.tensor_copy, wcu_bf, w_raw["wc"], 0, M, 0)
        interleave(nc.vector.tensor_copy, wcu_bf, w_raw["wu"], 0, M, M)

        gate_bank = [ps.tile([P, N], F32, name="gate_bank%d" % i) for i in range(G)]
        cand_bank = [ps.tile([P, N], F32, name="cand_bank%d" % i) for i in range(G)]

        def head_rows(i):
            return slice(ROWS * ORDER[i], ROWS * (ORDER[i] + 1))

        def product(bank, name, i):
            rows = head_rows(i)
            nc.tensor.matmul_mx(
                out=bank[i][:],
                lhsT=w_codes[rows, w_cols[name]].bitcast(FP8X4),
                lhsT_scale=w_scales[rows, w_cols[name]],
                rhs=h_codes[rows, :].bitcast(FP8X4),
                rhs_scale=h_scales[rows, :],
                start=True,
                stop=True,
            )

        product(gate_bank, "wr", 0)
        product(gate_bank, "wr", 1)
        quantize(w_codes, w_scales, wcu_bf, M, 2 * M, 0)
        nc.vector.transpose(out=bias_cols[:], in_=bias_rows[:])
        product(cand_bank, "wc", 0)
        product(cand_bank, "wc", 1)
        product(gate_bank, "wr", 2)

        r_sum, r, u_sum = per_turn("r_sum"), per_turn("r"), per_turn("u_sum")
        gated, c_sum = per_turn("gated"), per_turn("c_sum")
        u_cand = per_turn("u_cand", 2 * N)
        u = [t[:, 0:N] for t in u_cand]
        cand = [t[:, N : 2 * N] for t in u_cand]
        kept, fresh, y = per_turn("kept", LATE), per_turn("fresh", LATE), per_turn("y", LATE)
        y_round = per_turn("y_round", LATE, BF16)
        moved_early = tile("moved_early", [P, PACK, EARLY], BF16)
        moved_mid = tile("moved_mid", [P, PACK, LATE - EARLY], BF16)
        u_cand_late = tile("u_cand_late", [P, PACK, 2, N - LATE], F32)

        def reset_gate(i):
            nc.vector.tensor_tensor(out=r_sum[i][:], in0=gate_bank[i][:], in1=x_sb["xr"][i][:], op=ALU.add)
            nc.scalar.activation(out=r[i][:], in_=r_sum[i][:], func=ACT.Sigmoid)

        def update_gate(i):
            nc.vector.tensor_tensor(out=u_sum[i][:], in0=gate_bank[i][:], in1=x_sb["xu"][i][:], op=ALU.add)
            nc.scalar.activation(out=u[i], in_=u_sum[i][:], func=ACT.Sigmoid)

        def apply_reset(i):
            column = QUAD * ORDER[i]
            nc.vector.scalar_tensor_tensor(
                out=gated[i][:], in0=cand_bank[i][:], scalar=bias_cols[:, column : column + 1],
                in1=r[i][:], op0=ALU.add, op1=ALU.mult,
            )

        def candidate_sum(engine, i, c0=0, c1=N):
            engine.tensor_tensor(out=c_sum[i][:, c0:c1], in0=gated[i][:, c0:c1], in1=x_sb["xc"][i][:, c0:c1], op=ALU.add)

        def candidate(i):
            nc.scalar.activation(out=cand[i], in_=c_sum[i][:], func=ACT.Tanh)

        def kept_part(out, u_part, hp_part):
            nc.vector.tensor_tensor(out=out, in0=u_part, in1=hp_part, op=ALU.mult)

        def fresh_part(out, u_part, cand_part):
            nc.vector.scalar_tensor_tensor(
                out=out, in0=u_part, scalar=1.0, in1=cand_part, op0=ALU.subtract, op1=ALU.mult
            )

        def keep(i, c0, c1):
            kept_part(kept[i][:, c0:c1], u[i][:, c0:c1], hp_sb[i][:, c0:c1])

        def renew(i, c0, c1):
            fresh_part(fresh[i][:, c0:c1], u[i][:, c0:c1], cand[i][:, c0:c1])

        def mix(engine, i, c0, c1):
            engine.tensor_tensor(out=y[i][:, c0:c1], in0=kept[i][:, c0:c1], in1=fresh[i][:, c0:c1], op=ALU.subtract)

        def round_y(i, c0, c1):
            nc.scalar.copy(out=y_round[i][:, c0:c1], in_=y[i][:, c0:c1])

        def move_early(i):
            nc.sync.dma_start(out=moved_early[head_rows(i), :, :], in_=y_round[i][:, 0:EARLY])

        def move_mid(i):
            nc.sync.dma_start(out=moved_mid[head_rows(i), :, :], in_=y_round[i][:, EARLY:LATE])

        def move_late(i):
            nc.sync.dma_start(
                out=u_cand_late[head_rows(i), :, :, :].rearrange("p x k n -> p (x k) n"),
                in_=u_cand[i][:].rearrange("m (k n) -> m k n", k=2)[:, :, LATE:N],
            )

        def store(i, queue=nc.sync):
            queue.dma_start(out=out_0[M * ORDER[i] : M * (ORDER[i] + 1), 0:LATE], in_=y[i][:])

        reset_gate(0)
        reset_gate(1)
        quantize(w_codes, w_scales, wcu_bf, 2 * M, 3 * M, M)
        product(gate_bank, "wu", 0)
        product(gate_bank, "wr", 3)
        product(gate_bank, "wu", 1)
        product(cand_bank, "wc", 2)
        product(cand_bank, "wc", 3)
        apply_reset(0)

        candidate_sum(nc.gpsimd, 0)
        apply_reset(1)
        update_gate(0)
        candidate(0)
        move_late(0)
        reset_gate(2)
        product(gate_bank, "wu", 2)

        candidate_sum(nc.vector, 1, 0, 320)
        keep(0, 0, LATE)
        renew(0, 0, LATE)

        mix(nc.gpsimd, 0, 0, LATE)
        candidate_sum(nc.gpsimd, 1, 320, N)
        reset_gate(3)
        product(gate_bank, "wu", 3)
        update_gate(1)
        candidate(1)
        move_late(1)
        round_y(0, 0, LATE)
        nc.scalar.dma_start(out=hp_sb[3][:], in_=hp[ORDER[3], :, 0:LATE])
        nc.scalar.dma_start(out=hp_late[:], in_=hp.rearrange("g (p x) n -> (g p) x n", x=PACK)[:, :, LATE:N])
        move_early(0)
        move_mid(0)
        apply_reset(2)
        candidate_sum(nc.gpsimd, 2)
        update_gate(2)
        candidate(2)
        move_late(2)
        apply_reset(3)
        update_gate(3)

        candidate_sum(nc.vector, 3)
        candidate(3)
        move_late(3)
        store(0, nc.scalar)
        keep(1, 0, LATE)
        renew(1, 0, LATE)
        keep(2, 0, EARLY)
        mix(nc.vector, 1, 0, LATE)
        round_y(1, 0, LATE)
        move_early(1)
        move_mid(1)
        keep(3, 0, EARLY)
        last_turns = (G - 2, G - 1)
        for i in last_turns:
            renew(i, 0, EARLY)
        for i in last_turns:
            mix(nc.vector, i, 0, EARLY)
            round_y(i, 0, EARLY)
            move_early(i)
        store(1)
        for step in (keep, renew):
            for i in last_turns:
                step(i, EARLY, LATE)
        for i in last_turns:
            mix(nc.vector, i, EARLY, LATE)
            round_y(i, EARLY, LATE)
            move_mid(i)
        for i in last_turns:
            store(i)

        kept_late = tile("kept_late", [P, PACK, N - LATE], F32)
        fresh_late = tile("fresh_late", [P, PACK, N - LATE], F32)
        y_late = tile("y_late", [P, PACK, N - LATE], F32)
        u_late, cand_late = u_cand_late[:, :, 0, :], u_cand_late[:, :, 1, :]
        halves = [slice(0, (N - LATE) // 2), slice((N - LATE) // 2, N - LATE)]
        fresh_part(fresh_late[:], u_late, cand_late)
        for cols in halves:
            kept_part(kept_late[:, :, cols], u_late[:, :, cols], hp_late[:, :, cols])
        for cols in halves:
            nc.vector.tensor_tensor(
                out=y_late[:, :, cols], in0=kept_late[:, :, cols], in1=fresh_late[:, :, cols], op=ALU.subtract
            )
        nc.sync.dma_start(out=out_0.rearrange("(q x) n -> q x n", x=PACK)[:, :, LATE:N], in_=y_late[:])

        early_bf = tile("early_bf", [P, PACK * EARLY], BF16)
        mid_bf = tile("mid_bf", [P, PACK * (LATE - EARLY)], BF16)
        late_bf = tile("late_bf", [P, PACK * (N - LATE)], BF16)
        y_codes = tile("y_codes", [P, N], U32)
        y_scales = tile("y_scales", [P, N], U8)
        words = out_1.rearrange("s p n x -> (s p) (n x)").bitcast(I32)
        scale_rows = out_2.rearrange("s f n -> (s f) n").bitcast(I32)

        interleave(nc.scalar.copy, early_bf, moved_early, 0, EARLY, 0)
        for cols in halves:
            interleave(nc.vector.tensor_copy, late_bf, y_late, cols.start, cols.stop, cols.start)
        interleave(nc.vector.tensor_copy, mid_bf, moved_mid, 0, LATE - EARLY, 0)
        for grouped, c0, c1 in ((late_bf, LATE, N), (mid_bf, EARLY, LATE), (early_bf, 0, EARLY)):
            quantize(y_codes, y_scales, grouped, c0, c1, 0)
            nc.sync.dma_start(out=words[:, c0:c1], in_=y_codes[:, c0:c1].bitcast(I32))
        blocks = QUAD * PACK // 32
        for q in range(P // QUAD):
            queue = nc.scalar if q < 2 else nc.sync
            queue.dma_start(
                out=scale_rows[blocks * q : blocks * (q + 1), :],
                in_=y_scales[QUAD * q : QUAD * q + blocks, :].bitcast(I32),
            )
